import numpy as np
import ml_dtypes


def mxq(x, axis, fmt="e4m3"):
    dtype, down = {"e4m3": (ml_dtypes.float8_e4m3fn, 7), "e5m2": (ml_dtypes.float8_e5m2, 14)}[fmt]
    v = np.moveaxis(np.asarray(x, np.float32).astype(ml_dtypes.bfloat16).astype(np.float64), axis, -1)
    blocks = v.reshape(v.shape[:-1] + (-1, 32))
    amax = np.abs(blocks).max(-1, keepdims=True)
    byte = np.maximum(np.where(amax > 0, np.frexp(amax)[1] - 1 + 127, 0) - down, 1)
    scale = np.exp2(byte - 127.0)
    codes = (blocks / scale).astype(np.float32).astype(dtype).astype(np.float64)
    return np.moveaxis((codes * scale).reshape(v.shape), -1, axis)


WIDE = False


def mx_kscale(k):
    if not WIDE:
        return np.ones(k)
    levels = np.array([10, -10, 5, -5, 0])
    if k % 512:
        return np.exp2(np.random.permutation(np.resize(levels, k // 32))).repeat(32)
    a = np.empty((k // 512, 16))
    for p in range(k // 512):
        a[p, :8] = np.random.permutation(np.resize(levels, 8))
        for g in range(8):
            far = levels[np.abs(levels - a[p, g]) >= 10]
            a[p, g + 8] = far[np.random.randint(len(far))]
    return np.exp2(a.ravel()).repeat(32)


def f64(x):
    return np.asarray(x).astype(np.float64)


def striped(idx):
    return np.tile(idx.reshape(-1, 16).T, (8, 1)).astype(np.uint16)


def unstriped(offs):
    return offs[:16].T.reshape(-1).astype(np.int64)


E2M1 = np.array([0.0, 0.5, 1.0, 1.5, 2.0, 3.0, 4.0, 6.0, -0.0, -0.5, -1.0, -1.5, -2.0, -3.0, -4.0, -6.0])


def pack_weight(w, fmt):
    k, n = w.shape
    w = f64(np.asarray(w, np.float32).astype(ml_dtypes.bfloat16)).reshape(k // 32, 32, n)
    amax = np.abs(w).max(1)
    if fmt == "e4m3":
        byte = np.frexp(amax)[1] - 1 + 127 - 7
    else:
        mant, ex = np.frexp(amax / 6.0)
        byte = np.where(mant > 0.5, ex, ex - 1) + 127
    byte = np.clip(np.where(amax > 0, byte, 1), 1, 254)
    scaled = (w * np.exp2(127.0 - byte)[:, None, :]).reshape(k, n).astype(np.float32)
    by_word = np.ascontiguousarray(scaled.reshape(k // 512, 128, 4, n).transpose(0, 1, 3, 2))
    if fmt == "e4m3":
        words = by_word.astype(ml_dtypes.float8_e4m3fn).view(np.uint8)
    else:
        c = by_word.astype(ml_dtypes.float4_e2m1fn).view(np.uint8) & 0xF
        words = (c[..., 0::2] | (c[..., 1::2] << 4)).reshape(k // 512, 128, 2 * n)
    return np.ascontiguousarray(words), np.ascontiguousarray(byte.astype(np.uint8).reshape(k // 512, 16, n))


def unpack_weight(words, scales, fmt):
    g, _, n = scales.shape
    words = np.ascontiguousarray(words).reshape(g, 128, n, -1)
    if fmt == "e4m3":
        vals = words.view(ml_dtypes.float8_e4m3fn).astype(np.float64)
    else:
        nib = np.empty((g, 128, n, 4), np.uint8)
        nib[..., 0::2] = words & 0xF
        nib[..., 1::2] = words >> 4
        vals = E2M1[nib]
    vals = vals * np.repeat(np.exp2(scales.astype(np.float64) - 127.0), 8, axis=1)[..., None]
    return vals.transpose(0, 1, 3, 2).reshape(g * 512, n)


def gelu(v):
    return 0.5 * v * (1.0 + np.tanh(np.sqrt(2.0 / np.pi) * (v + 0.044715 * v**3)))


K, T, E, N = 2560, 640, 8, 256
COUNTS = (128, 128, 128, 128, 128, 256, 256, 128)
STARTS = np.cumsum((0,) + COUNTS)
K8 = 1024


def by_expert(wq, xq):
    return np.concatenate([wq[e].T @ xq[:, STARTS[e]:STARTS[e + 1]] for e in range(E)], axis=1)


def setup_inputs():
    n = np.random.standard_normal
    s = mx_kscale(K)[:, None]
    both = np.repeat(np.arange(E), COUNTS)
    pair = np.stack([both[:T], both[T:]])[:, np.random.permutation(T)]
    pair = np.where(np.random.rand(T) < 0.5, pair, pair[::-1])
    for _ in range(8):
        s_, t_ = np.random.permutation(T).reshape(2, -1); r = np.random.randint(2, size=T // 2); q = np.random.randint(2, size=T // 2); x, y = pair[r, s_].copy(), pair[q, t_].copy()
        ok = (pair[1 - r, s_] != y) & (pair[1 - q, t_] != x); pair[r[ok], s_[ok]] = y[ok]; pair[q[ok], t_[ok]] = x[ok]
    order = np.argsort(pair.reshape(-1), kind="stable")
    slot_token = order % T; pos = np.empty(2 * T, np.int64); pos[order] = np.arange(2 * T); pos = pos.reshape(2, T)
    g = np.random.uniform(0.2, 0.8, T)
    w = n((E, K, N)) / np.sqrt(K) / s[None]
    w8 = [pack_weight(m[:K8], "e4m3") for m in w]
    w4 = [pack_weight(m[K8:], "e2m1") for m in w]
    return {
        "xT": (n((K, T)) * s).astype(np.float32),
        "w8_words": np.stack([m[0] for m in w8]),
        "w8_scales": np.stack([m[1] for m in w8]),
        "w4_words": np.stack([m[0] for m in w4]),
        "w4_scales": np.stack([m[1] for m in w4]),
        "b": (0.3 * n((N, E))).astype(np.float32),
        "gate": np.stack([np.tile(g, (N, 1)), np.tile(1.0 - g, (N, 1))]).astype(np.float32),
        "offs": striped(slot_token),
        "pos1": striped(pos[0]),
        "pos2": striped(pos[1]),
    }


def reference(xT, w8_words, w8_scales, w4_words, w4_scales, b, gate, offs, pos1, pos2):
    idx = unstriped(offs)
    w = np.stack([np.concatenate([unpack_weight(w8_words[e], w8_scales[e], "e4m3"), unpack_weight(w4_words[e], w4_scales[e], "e2m1")]) for e in range(E)])
    xq = mxq(f64(xT)[:, idx], 0, "e4m3")
    y = by_expert(w, xq)
    y = gelu(y + np.repeat(f64(b), COUNTS, axis=1))
    return f64(gate[0]) * y[:, unstriped(pos1)] + f64(gate[1]) * y[:, unstriped(pos2)]

@@ -1,0 +1,225 @@
+from contextlib import ExitStack
+
+import concourse.mybir as mybir
+
+P = 128
+K, T, E, N = 2560, 640, 8, 256
+COUNTS = (128, 128, 128, 128, 128, 256, 256, 128)
+SLOTS = 2 * T
+BLOCK = 128
+BLOCK_EXPERT = [e for e in range(E) for i in range(COUNTS[e] // BLOCK)]
+HALVES = N // P
+PASSES = K // 512
+PASSES8 = 2
+
+F32 = mybir.dt.float32
+BF16 = mybir.dt.bfloat16
+I32 = mybir.dt.int32
+U32 = mybir.dt.uint32
+U16 = mybir.dt.uint16
+U8 = mybir.dt.uint8
+FP8X4 = mybir.dt.float8_e4m3fn_x4
+FP4X4 = mybir.dt.float4_e2m1fn_x4
+COPY = mybir.ActivationFunctionType.Copy
+GELU = mybir.ActivationFunctionType.Gelu_apprx_tanh
+MULT = mybir.AluOpType.mult
+
+FLOPS = 2 * SLOTS * K * N
+
+ORDER = (2, 0, 1, 3, 4)
+ROW = {2: 0, 0: 4, 1: 8, 3: 12}
+MOVED = 3
+LAST = 4
+
+
+def tile_moe_rag_lin_gelu_kernel(
+    tc, xT, w8_words, w8_scales, w4_words, w4_scales, b, gate, offs, pos1, pos2, out
+):
+    nc = tc.nc
+    with ExitStack() as ctx:
+        lists = ctx.enter_context(tc.tile_pool(name="lists", bufs=1))
+        keep = ctx.enter_context(tc.tile_pool(name="keep", bufs=1))
+        psum = ctx.enter_context(tc.psum_pool(name="psum", bufs=8))
+
+        offs_t = lists.tile([P, SLOTS // 16], U16, name="offs_t")
+        pos1_t = lists.tile([P, T // 16], U16, name="pos1_t")
+        pos2_t = lists.tile([P, T // 16], U16, name="pos2_t")
+
+        warm = keep.tile([P, 8], F32, name="warm")
+        nc.vector.memset(warm[:], 0.0)
+        warmed = keep.tile([P, 8], F32, name="warmed")
+        nc.scalar.activation(warmed[:], warm[:], GELU)
+
+        packed = keep.tile([P, T], U8, name="packed", align_bytes=64)
+        nc.vector.memset(packed[:].bitcast(I32), 0)
+        lastp = keep.tile([P, T], U8, name="lastp", align_bytes=64)
+        nc.vector.memset(lastp[:].bitcast(I32), 0)
+        gmoved = keep.tile([P, SLOTS], U8, name="gmoved", align_bytes=64)
+        nc.vector.memset(gmoved[:].bitcast(I32), 0)
+        w8s = keep.tile([P, E * PASSES8, N], U8, name="w8s", align_bytes=64)
+        w4s = keep.tile([P, E * (PASSES - PASSES8), N], U8, name="w4s", align_bytes=64)
+        nc.vector.memset(w8s[:].bitcast(I32), 0)
+        nc.vector.memset(w4s[:].bitcast(I32), 0)
+
+        raw = {a: keep.tile([P, 4, T], F32, name=f"raw{a}") for a in ORDER}
+        xv = xT.rearrange("(a p j) t -> a p j t", p=P, j=4)
+        first = ORDER[0]
+        nc.sync.dma_start(raw[first][:, :, 0:256], xv[first, :, :, 0:256])
+        nc.sync.dma_start(raw[first][:, :, 256:512], xv[first, :, :, 256:512])
+        nc.sync.dma_start(raw[first][:, :, 512:T], xv[first, :, :, 512:T])
+        nc.sync.dma_start(offs_t[:], offs)
+        for a in ORDER[1:]:
+            nc.sync.dma_start(raw[a][:], xv[a])
+        bias = keep.tile([P, HALVES, E], F32, name="bias")
+        nc.scalar.dma_start(bias[:], b.rearrange("(h p) e -> p h e", p=P))
+        s8v = w8_scales.rearrange("e a q n -> q (e a) n")
+        s4v = w4_scales.rearrange("e a q n -> q (e a) n")
+        for q in range(4):
+            nc.sync.dma_start(w8s[32 * q : 32 * q + 4, :, :].bitcast(I32), s8v[4 * q : 4 * q + 4, :, :].bitcast(I32))
+        for q in range(4):
+            nc.sync.dma_start(w4s[32 * q : 32 * q + 4, :, :].bitcast(I32), s4v[4 * q : 4 * q + 4, :, :].bitcast(I32))
+        v8 = w8_words.rearrange("e a p n r -> p (e a) (n r)")
+        v4 = w4_words.rearrange("e a p m -> p (e a) m")
+        w8, w4 = [], []
+        for g in range(E // 2):
+            t8 = keep.tile([P, 4, 4 * N], U8, name=f"w8_{g}", align_bytes=64)
+            nc.sync.dma_start(t8[:].bitcast(I32), v8[:, 4 * g : 4 * g + 4, :].bitcast(I32))
+            t4 = keep.tile([P, 6, 2 * N], U8, name=f"w4_{g}", align_bytes=64)
+            nc.sync.dma_start(t4[:].bitcast(I32), v4[:, 6 * g : 6 * g + 6, :].bitcast(I32))
+            w8.append(t8)
+            w4.append(t4)
+        nc.sync.dma_start(pos1_t[:], pos1)
+        nc.sync.dma_start(pos2_t[:], pos2)
+        gates = {}
+        for h in range(HALVES):
+            for c in range(2):
+                gates[c, h] = keep.tile([P, T], F32, name=f"gate{c}{h}")
+                nc.sync.dma_start(gates[c, h][:], gate[c, h * P : (h + 1) * P, :])
+
+        xb = {a: keep.tile([P, T, 4], BF16, name=f"xb{a}", align_bytes=64) for a in ORDER}
+        words = {a: keep.tile([P, T], U32, name=f"words{a}", align_bytes=64) for a in ORDER}
+        gwords = {a: keep.tile([P, SLOTS], U32, name=f"gwords{a}", align_bytes=64) for a in ORDER}
+        gpacked = keep.tile([P, SLOTS], U8, name="gpacked", align_bytes=64)
+        glast = keep.tile([P, SLOTS], U8, name="glast", align_bytes=64)
+
+        def cast(a, lo, hi, vector=False):
+            dst = xb[a][:, lo:hi, :].rearrange("p (c i) t -> p c t i", i=4)
+            src = raw[a][:, :, lo:hi].rearrange("p t (c i) -> p c t i", i=4)
+            if vector:
+                nc.vector.tensor_copy(dst, src)
+            else:
+                nc.scalar.activation(dst, src, COPY)
+
+        def quant(a, lo, hi):
+            scales = lastp[:, lo:hi] if a == LAST else packed[ROW[a] : P, lo:hi]
+            nc.vector.quantize_mx(
+                words[a][:, lo:hi].bitcast(FP8X4), scales, xb[a][:, lo:hi, :].rearrange("p c t -> p (c t)")
+            )
+
+        def gather(dst, window, lo, hi):
+            nc.vector.tensor_copy(dst[:, lo:hi], window[:].indirect(offs_t[:, lo // 16 : hi // 16]))
+
+        thirds = ((0, 480), (480, 960), (960, 1280))
+
+        def gw(a, i):
+            gather(gwords[a], words[a], thirds[i][0], thirds[i][1])
+
+        def q(a):
+            quant(a, 0, 512)
+            quant(a, 512, T)
+
+        cast(first, 0, 256)
+        cast(first, 256, 512, vector=True)
+        cast(first, 512, T)
+        for a in ORDER[1:]:
+            cast(a, 0, 512)
+            cast(a, 512, T)
+
+        quant(first, 0, 256)
+        quant(first, 256, 512)
+        quant(first, 512, T)
+        gw(2, 0)
+        gw(2, 1)
+        q(0)
+        gw(2, 2)
+        gw(0, 0)
+        gw(0, 1)
+        q(1)
+        gw(0, 2)
+        gw(1, 0)
+        gw(1, 1)
+        q(3)
+        gw(1, 2)
+        for i in range(3):
+            gather(gpacked, packed, thirds[i][0], thirds[i][1])
+        nc.sync.dma_start(gmoved[0:112, :].bitcast(I32), gpacked[12:124, :].bitcast(I32))
+        q(4)
+
+        y = [keep.tile([P, SLOTS], F32, name=f"y{h}") for h in range(HALVES)]
+        acc = {}
+
+        def multiply(blk, h, a):
+            e = BLOCK_EXPERT[blk]
+            s = blk * BLOCK
+            cols = slice(s, s + BLOCK)
+            if a < PASSES8:
+                lhsT = w8[e // 2][:, PASSES8 * (e % 2) + a, 512 * h : 512 * (h + 1)].bitcast(FP8X4)
+                lhsT_scale = w8s[:, PASSES8 * e + a, h * P : (h + 1) * P]
+            else:
+                lhsT = w4[e // 2][:, 3 * (e % 2) + a - PASSES8, 256 * h : 256 * (h + 1)].bitcast(FP4X4)
+                lhsT_scale = w4s[:, 3 * e + a - PASSES8, h * P : (h + 1) * P]
+            if a == LAST:
+                rhs_scale = glast[:, cols]
+            elif a == MOVED:
+                rhs_scale = gmoved[:, cols]
+            else:
+                rhs_scale = gpacked[ROW[a] : P, cols]
+            nc.tensor.matmul_mx(
+                acc[blk, h][:],
+                lhsT=lhsT,
+                lhsT_scale=lhsT_scale,
+                rhs=gwords[a][:, cols].bitcast(FP8X4),
+                rhs_scale=rhs_scale,
+                start=(a == ORDER[0]),
+                stop=(a == LAST),
+            )
+
+        def begin(blk):
+            for h in range(HALVES):
+                acc[blk, h] = psum.tile([P, BLOCK], F32, name="acc")
+                for a in ORDER[:3]:
+                    multiply(blk, h, a)
+
+        def finish(blk):
+            e = BLOCK_EXPERT[blk]
+            for h in range(HALVES):
+                multiply(blk, h, MOVED)
+                multiply(blk, h, LAST)
+                s = blk * BLOCK
+                nc.scalar.activation(y[h][:, s : s + BLOCK], acc[blk, h][:], GELU, bias=bias[:, h, e : e + 1])
+
+        for blk in range(4):
+            begin(blk)
+        pieces = ((0, 384), (384, 768), (768, 1152), (1152, 1280))
+        opened = 4
+        for lo, hi in pieces:
+            gather(gwords[MOVED], words[MOVED], lo, hi)
+            gather(glast, lastp, lo, hi)
+            gather(gwords[LAST], words[LAST], lo, hi)
+            for blk in range(lo // BLOCK, hi // BLOCK):
+                finish(blk)
+            while opened < min(len(BLOCK_EXPERT), hi // BLOCK + 4):
+                begin(opened)
+                opened += 1
+
+        for h in range(HALVES):
+            prod1 = keep.tile([P, T], F32, name=f"prod1{h}")
+            prod2 = keep.tile([P, T], F32, name=f"prod2{h}")
+            res = keep.tile([P, T], F32, name=f"res{h}")
+            bounds = (0, T) if h == 0 else (0, 320, T)
+            for lo, hi in zip(bounds, bounds[1:]):
+                cols = slice(lo // 16, hi // 16)
+                nc.vector.tensor_tensor(prod1[:, lo:hi], y[h][:].indirect(pos1_t[:, cols]), gates[0, h][:, lo:hi], MULT)
+                nc.vector.tensor_tensor(prod2[:, lo:hi], y[h][:].indirect(pos2_t[:, cols]), gates[1, h][:, lo:hi], MULT)
+                nc.vector.tensor_add(res[:, lo:hi], prod1[:, lo:hi], prod2[:, lo:hi])
+                nc.sync.dma_start(out[h * P : (h + 1) * P, lo:hi], res[:, lo:hi])

@@ -26,10 +26,11 @@ MULT = mybir.AluOpType.mult
 
 FLOPS = 2 * SLOTS * K * N
 
-ORDER = (2, 0, 1, 3, 4)
-ROW = {2: 0, 0: 4, 1: 8, 3: 12}
+ORDER = (2, 3, 0, 4, 1)
+EARLY = (2, 0, 3)
+LATE = ORDER[3:]
+ROW = {2: 0, 0: 4, 3: 8, 4: 0, 1: 4}
 MOVED = 3
-LAST = 4
 
 
 def tile_moe_rag_lin_gelu_kernel(
@@ -65,19 +66,21 @@ def tile_moe_rag_lin_gelu_kernel(
         xv = xT.rearrange("(a p j) t -> a p j t", p=P, j=4)
         first = ORDER[0]
         nc.sync.dma_start(raw[first][:, :, 0:256], xv[first, :, :, 0:256])
-        nc.sync.dma_start(raw[first][:, :, 256:512], xv[first, :, :, 256:512])
-        nc.sync.dma_start(raw[first][:, :, 512:T], xv[first, :, :, 512:T])
+        nc.sync.dma_start(raw[first][:, :, 256:T], xv[first, :, :, 256:T])
         nc.sync.dma_start(offs_t[:], offs)
-        for a in ORDER[1:]:
+        second = ORDER[1]
+        nc.sync.dma_start(raw[second][:, :, 0:384], xv[second, :, :, 0:384])
+        nc.sync.dma_start(raw[second][:, :, 384:T], xv[second, :, :, 384:T])
+        for a in ORDER[2:]:
             nc.sync.dma_start(raw[a][:], xv[a])
         bias = keep.tile([P, HALVES, E], F32, name="bias")
         nc.scalar.dma_start(bias[:], b.rearrange("(h p) e -> p h e", p=P))
         s8v = w8_scales.rearrange("e a q n -> q (e a) n")
         s4v = w4_scales.rearrange("e a q n -> q (e a) n")
         for q in range(4):
-            nc.sync.dma_start(w8s[32 * q : 32 * q + 4, :, :].bitcast(I32), s8v[4 * q : 4 * q + 4, :, :].bitcast(I32))
+            nc.gpsimd.dma_start(w8s[32 * q : 32 * q + 4, :, :].bitcast(I32), s8v[4 * q : 4 * q + 4, :, :].bitcast(I32))
         for q in range(4):
-            nc.sync.dma_start(w4s[32 * q : 32 * q + 4, :, :].bitcast(I32), s4v[4 * q : 4 * q + 4, :, :].bitcast(I32))
+            nc.gpsimd.dma_start(w4s[32 * q : 32 * q + 4, :, :].bitcast(I32), s4v[4 * q : 4 * q + 4, :, :].bitcast(I32))
         v8 = w8_words.rearrange("e a p n r -> p (e a) (n r)")
         v4 = w4_words.rearrange("e a p m -> p (e a) m")
         w8, w4 = [], []
@@ -111,7 +114,7 @@ def tile_moe_rag_lin_gelu_kernel(
                 nc.scalar.activation(dst, src, COPY)
 
         def quant(a, lo, hi):
-            scales = lastp[:, lo:hi] if a == LAST else packed[ROW[a] : P, lo:hi]
+            scales = (packed if a in EARLY else lastp)[ROW[a] : P, lo:hi]
             nc.vector.quantize_mx(
                 words[a][:, lo:hi].bitcast(FP8X4), scales, xb[a][:, lo:hi, :].rearrange("p c t -> p (c t)")
             )
@@ -131,29 +134,32 @@ def tile_moe_rag_lin_gelu_kernel(
         cast(first, 0, 256)
         cast(first, 256, 512, vector=True)
         cast(first, 512, T)
-        for a in ORDER[1:]:
+        cast(second, 0, 384)
+        cast(second, 384, 512)
+        for a in ORDER[2:]:
             cast(a, 0, 512)
             cast(a, 512, T)
 
-        quant(first, 0, 256)
-        quant(first, 256, 512)
-        quant(first, 512, T)
+        quant(2, 0, 256)
+        quant(2, 256, 512)
+        quant(2, 512, T)
         gw(2, 0)
         gw(2, 1)
-        q(0)
+        cast(second, 512, T, vector=True)
+        q(3)
         gw(2, 2)
+        gw(3, 0)
+        gw(3, 1)
+        q(0)
+        gw(3, 2)
+        for i in range(3):
+            gather(gpacked, packed, thirds[i][0], thirds[i][1])
+        nc.scalar.dma_start(gmoved[0:112, :].bitcast(I32), gpacked[8:120, :].bitcast(I32))
+        q(4)
         gw(0, 0)
         gw(0, 1)
         q(1)
         gw(0, 2)
-        gw(1, 0)
-        gw(1, 1)
-        q(3)
-        gw(1, 2)
-        for i in range(3):
-            gather(gpacked, packed, thirds[i][0], thirds[i][1])
-        nc.sync.dma_start(gmoved[0:112, :].bitcast(I32), gpacked[12:124, :].bitcast(I32))
-        q(4)
 
         y = [keep.tile([P, SLOTS], F32, name=f"y{h}") for h in range(HALVES)]
         acc = {}
@@ -168,33 +174,31 @@ def tile_moe_rag_lin_gelu_kernel(
             else:
                 lhsT = w4[e // 2][:, 3 * (e % 2) + a - PASSES8, 256 * h : 256 * (h + 1)].bitcast(FP4X4)
                 lhsT_scale = w4s[:, 3 * e + a - PASSES8, h * P : (h + 1) * P]
-            if a == LAST:
-                rhs_scale = glast[:, cols]
-            elif a == MOVED:
+            if a == MOVED:
                 rhs_scale = gmoved[:, cols]
             else:
-                rhs_scale = gpacked[ROW[a] : P, cols]
+                rhs_scale = (gpacked if a in EARLY else glast)[ROW[a] : P, cols]
             nc.tensor.matmul_mx(
                 acc[blk, h][:],
                 lhsT=lhsT,
                 lhsT_scale=lhsT_scale,
                 rhs=gwords[a][:, cols].bitcast(FP8X4),
                 rhs_scale=rhs_scale,
-                start=(a == ORDER[0]),
-                stop=(a == LAST),
+                start=(a == EARLY[0]),
+                stop=(a == ORDER[-1]),
             )
 
         def begin(blk):
             for h in range(HALVES):
                 acc[blk, h] = psum.tile([P, BLOCK], F32, name="acc")
-                for a in ORDER[:3]:
+                for a in EARLY:
                     multiply(blk, h, a)
 
         def finish(blk):
             e = BLOCK_EXPERT[blk]
             for h in range(HALVES):
-                multiply(blk, h, MOVED)
-                multiply(blk, h, LAST)
+                for a in LATE:
+                    multiply(blk, h, a)
                 s = blk * BLOCK
                 nc.scalar.activation(y[h][:, s : s + BLOCK], acc[blk, h][:], GELU, bias=bias[:, h, e : e + 1])
 
@@ -203,9 +207,9 @@ def tile_moe_rag_lin_gelu_kernel(
         pieces = ((0, 384), (384, 768), (768, 1152), (1152, 1280))
         opened = 4
         for lo, hi in pieces:
-            gather(gwords[MOVED], words[MOVED], lo, hi)
             gather(glast, lastp, lo, hi)
-            gather(gwords[LAST], words[LAST], lo, hi)
+            for a in LATE:
+                gather(gwords[a], words[a], lo, hi)
             for blk in range(lo // BLOCK, hi // BLOCK):
                 finish(blk)
             while opened < min(len(BLOCK_EXPERT), hi // BLOCK + 4):

@@ -46,6 +46,17 @@ def tile_moe_rag_lin_gelu_kernel(
         pos1_t = lists.tile([P, T // 16], U16, name="pos1_t")
         pos2_t = lists.tile([P, T // 16], U16, name="pos2_t")
 
+        w4s = keep.tile([P, E * (PASSES - PASSES8), N], U8, name="w4s", align_bytes=64)
+        w8s = keep.tile([P, E * PASSES8, N], U8, name="w8s", align_bytes=64)
+        nc.vector.memset(w4s[:].bitcast(I32), 0)
+        nc.vector.memset(w8s[:].bitcast(I32), 0)
+        s8v = w8_scales.rearrange("e a q n -> q (e a) n")
+        s4v = w4_scales.rearrange("e a q n -> q (e a) n")
+        for q in range(4):
+            nc.gpsimd.dma_start(w4s[32 * q : 32 * q + 4, :, :].bitcast(I32), s4v[4 * q : 4 * q + 4, :, :].bitcast(I32))
+        for q in range(4):
+            nc.gpsimd.dma_start(w8s[32 * q : 32 * q + 4, :, :].bitcast(I32), s8v[4 * q : 4 * q + 4, :, :].bitcast(I32))
+
         warm = keep.tile([P, 8], F32, name="warm")
         nc.vector.memset(warm[:], 0.0)
         warmed = keep.tile([P, 8], F32, name="warmed")
@@ -57,40 +68,33 @@ def tile_moe_rag_lin_gelu_kernel(
         nc.vector.memset(lastp[:].bitcast(I32), 0)
         gmoved = keep.tile([P, SLOTS], U8, name="gmoved", align_bytes=64)
         nc.vector.memset(gmoved[:].bitcast(I32), 0)
-        w8s = keep.tile([P, E * PASSES8, N], U8, name="w8s", align_bytes=64)
-        w4s = keep.tile([P, E * (PASSES - PASSES8), N], U8, name="w4s", align_bytes=64)
-        nc.vector.memset(w8s[:].bitcast(I32), 0)
-        nc.vector.memset(w4s[:].bitcast(I32), 0)
 
         raw = {a: keep.tile([P, 4, T], F32, name=f"raw{a}") for a in ORDER}
         xv = xT.rearrange("(a p j) t -> a p j t", p=P, j=4)
-        first = ORDER[0]
-        nc.sync.dma_start(raw[first][:, :, 0:256], xv[first, :, :, 0:256])
-        nc.sync.dma_start(raw[first][:, :, 256:T], xv[first, :, :, 256:T])
-        nc.sync.dma_start(offs_t[:], offs)
-        second = ORDER[1]
-        nc.sync.dma_start(raw[second][:, :, 0:384], xv[second, :, :, 0:384])
-        nc.sync.dma_start(raw[second][:, :, 384:T], xv[second, :, :, 384:T])
-        for a in ORDER[2:]:
-            nc.sync.dma_start(raw[a][:], xv[a])
-        bias = keep.tile([P, HALVES, E], F32, name="bias")
-        nc.scalar.dma_start(bias[:], b.rearrange("(h p) e -> p h e", p=P))
-        s8v = w8_scales.rearrange("e a q n -> q (e a) n")
-        s4v = w4_scales.rearrange("e a q n -> q (e a) n")
-        for q in range(4):
-            nc.gpsimd.dma_start(w8s[32 * q : 32 * q + 4, :, :].bitcast(I32), s8v[4 * q : 4 * q + 4, :, :].bitcast(I32))
-        for q in range(4):
-            nc.gpsimd.dma_start(w4s[32 * q : 32 * q + 4, :, :].bitcast(I32), s4v[4 * q : 4 * q + 4, :, :].bitcast(I32))
         v8 = w8_words.rearrange("e a p n r -> p (e a) (n r)")
         v4 = w4_words.rearrange("e a p m -> p (e a) m")
-        w8, w4 = [], []
-        for g in range(E // 2):
-            t8 = keep.tile([P, 4, 4 * N], U8, name=f"w8_{g}", align_bytes=64)
-            nc.sync.dma_start(t8[:].bitcast(I32), v8[:, 4 * g : 4 * g + 4, :].bitcast(I32))
-            t4 = keep.tile([P, 6, 2 * N], U8, name=f"w4_{g}", align_bytes=64)
-            nc.sync.dma_start(t4[:].bitcast(I32), v4[:, 6 * g : 6 * g + 6, :].bitcast(I32))
-            w8.append(t8)
-            w4.append(t4)
+        w8 = [keep.tile([P, 4, 4 * N], U8, name=f"w8_{g}", align_bytes=64) for g in range(E // 2)]
+        w4 = [keep.tile([P, 6, 2 * N], U8, name=f"w4_{g}", align_bytes=64) for g in range(E // 2)]
+        bias = keep.tile([P, HALVES, E], F32, name="bias")
+
+        def load_x(a):
+            nc.sync.dma_start(raw[a][:], xv[a])
+
+        def load_w(g):
+            nc.sync.dma_start(w8[g][:].bitcast(I32), v8[:, 4 * g : 4 * g + 4, :].bitcast(I32))
+            nc.sync.dma_start(w4[g][:].bitcast(I32), v4[:, 6 * g : 6 * g + 6, :].bitcast(I32))
+
+        load_x(2)
+        nc.sync.dma_start(offs_t[:], offs)
+        load_x(3)
+        load_x(0)
+        load_w(0)
+        load_x(4)
+        load_x(1)
+        load_w(1)
+        load_w(2)
+        load_w(3)
+        nc.sync.dma_start(bias[:], b.rearrange("(h p) e -> p h e", p=P))
         nc.sync.dma_start(pos1_t[:], pos1)
         nc.sync.dma_start(pos2_t[:], pos2)
         gates = {}
@@ -131,35 +135,47 @@ def tile_moe_rag_lin_gelu_kernel(
             quant(a, 0, 512)
             quant(a, 512, T)
 
-        cast(first, 0, 256)
-        cast(first, 256, 512, vector=True)
-        cast(first, 512, T)
-        cast(second, 0, 384)
-        cast(second, 384, 512)
-        for a in ORDER[2:]:
+        pieces = ((0, 384), (384, 768), (768, 1152), (1152, 1280))
+
+        def gp(a, i):
+            gather(gwords[a], words[a], pieces[i][0], pieces[i][1])
+
+        cast(2, 0, 256)
+        cast(2, 512, T, vector=True)
+        cast(2, 256, 512, vector=True)
+        cast(3, 0, 256)
+        cast(3, 256, 512)
+        for a in (0, 4):
             cast(a, 0, 512)
             cast(a, 512, T)
 
-        quant(2, 0, 256)
-        quant(2, 256, 512)
         quant(2, 512, T)
+        quant(2, 256, 512)
+        quant(2, 0, 256)
         gw(2, 0)
         gw(2, 1)
-        cast(second, 512, T, vector=True)
-        q(3)
+        cast(3, 512, T, vector=True)
         gw(2, 2)
+        quant(3, 512, T)
+        quant(3, 0, 512)
         gw(3, 0)
         gw(3, 1)
-        q(0)
+        quant(0, 0, 512)
         gw(3, 2)
+        quant(0, 512, T)
         for i in range(3):
             gather(gpacked, packed, thirds[i][0], thirds[i][1])
         nc.scalar.dma_start(gmoved[0:112, :].bitcast(I32), gpacked[8:120, :].bitcast(I32))
-        q(4)
+        cast(1, 0, 512)
+        cast(1, 512, T)
         gw(0, 0)
         gw(0, 1)
-        q(1)
+        q(4)
         gw(0, 2)
+        gp(4, 0)
+        gp(4, 1)
+        q(1)
+        gp(4, 3)
 
         y = [keep.tile([P, SLOTS], F32, name=f"y{h}") for h in range(HALVES)]
         acc = {}
@@ -204,26 +220,39 @@ def tile_moe_rag_lin_gelu_kernel(
 
         for blk in range(4):
             begin(blk)
-        pieces = ((0, 384), (384, 768), (768, 1152), (1152, 1280))
         opened = 4
-        for lo, hi in pieces:
+        for i, (lo, hi) in enumerate(pieces):
+            if i == 2:
+                gp(4, 2)
             gather(glast, lastp, lo, hi)
-            for a in LATE:
-                gather(gwords[a], words[a], lo, hi)
+            gp(1, i)
             for blk in range(lo // BLOCK, hi // BLOCK):
                 finish(blk)
             while opened < min(len(BLOCK_EXPERT), hi // BLOCK + 4):
                 begin(opened)
                 opened += 1
 
-        for h in range(HALVES):
-            prod1 = keep.tile([P, T], F32, name=f"prod1{h}")
-            prod2 = keep.tile([P, T], F32, name=f"prod2{h}")
-            res = keep.tile([P, T], F32, name=f"res{h}")
-            bounds = (0, T) if h == 0 else (0, 320, T)
-            for lo, hi in zip(bounds, bounds[1:]):
-                cols = slice(lo // 16, hi // 16)
-                nc.vector.tensor_tensor(prod1[:, lo:hi], y[h][:].indirect(pos1_t[:, cols]), gates[0, h][:, lo:hi], MULT)
-                nc.vector.tensor_tensor(prod2[:, lo:hi], y[h][:].indirect(pos2_t[:, cols]), gates[1, h][:, lo:hi], MULT)
-                nc.vector.tensor_add(res[:, lo:hi], prod1[:, lo:hi], prod2[:, lo:hi])
-                nc.sync.dma_start(out[h * P : (h + 1) * P, lo:hi], res[:, lo:hi])
+        spans = ((0, 0, T), (1, 0, 320), (1, 320, T))
+        prods = {}
+
+        def product(i, c):
+            h, lo, hi = spans[i]
+            prods[i, c] = keep.tile([P, hi - lo], F32, name=f"prod{i}{c}")
+            pos = (pos1_t, pos2_t)[c]
+            nc.vector.tensor_tensor(prods[i, c][:], y[h][:].indirect(pos[:, lo // 16 : hi // 16]), gates[c, h][:, lo:hi], MULT)
+
+        def combine(i):
+            h, lo, hi = spans[i]
+            res = keep.tile([P, hi - lo], F32, name=f"res{i}")
+            nc.vector.tensor_add(res[:], prods[i, 0][:], prods[i, 1][:])
+            nc.sync.dma_start(out[h * P : (h + 1) * P, lo:hi], res[:])
+
+        product(0, 0)
+        product(0, 1)
+        product(1, 0)
+        combine(0)
+        product(1, 1)
+        product(2, 0)
+        combine(1)
+        product(2, 1)
+        combine(2)

@@ -27,9 +27,9 @@ MULT = mybir.AluOpType.mult
 FLOPS = 2 * SLOTS * K * N
 
 ORDER = (2, 3, 0, 4, 1)
-EARLY = (2, 0, 3)
-LATE = ORDER[3:]
-ROW = {2: 0, 0: 4, 3: 8, 4: 0, 1: 4}
+EARLY = ORDER[:2]
+LATE = ORDER[2:]
+ROW = {2: 0, 3: 8, 4: 0, 0: 4, 1: 8}
 MOVED = 3
 
 
@@ -54,6 +54,7 @@ def tile_moe_rag_lin_gelu_kernel(
         s4v = w4_scales.rearrange("e a q n -> q (e a) n")
         for q in range(4):
             nc.gpsimd.dma_start(w4s[32 * q : 32 * q + 4, :, :].bitcast(I32), s4v[4 * q : 4 * q + 4, :, :].bitcast(I32))
+
         for q in range(4):
             nc.gpsimd.dma_start(w8s[32 * q : 32 * q + 4, :, :].bitcast(I32), s8v[4 * q : 4 * q + 4, :, :].bitcast(I32))
 
@@ -73,34 +74,49 @@ def tile_moe_rag_lin_gelu_kernel(
         xv = xT.rearrange("(a p j) t -> a p j t", p=P, j=4)
         v8 = w8_words.rearrange("e a p n r -> p (e a) (n r)")
         v4 = w4_words.rearrange("e a p m -> p (e a) m")
-        w8 = [keep.tile([P, 4, 4 * N], U8, name=f"w8_{g}", align_bytes=64) for g in range(E // 2)]
-        w4 = [keep.tile([P, 6, 2 * N], U8, name=f"w4_{g}", align_bytes=64) for g in range(E // 2)]
-        bias = keep.tile([P, HALVES, E], F32, name="bias")
+        groups8 = ((0, 2), (2, 4), (4, 5), (5, 6), (6, 7), (7, 8))
+        groups4 = ((0, 2), (2, 4), (4, 5), (5, 6), (6, 7), (7, 8))
+        w8 = [keep.tile([P, 2 * (hi - lo), 4 * N], U8, name=f"w8_{lo}", align_bytes=64) for lo, hi in groups8]
+        w4 = [keep.tile([P, 3 * (hi - lo), 2 * N], U8, name=f"w4_{lo}", align_bytes=64) for lo, hi in groups4]
 
-        def load_x(a):
-            nc.sync.dma_start(raw[a][:], xv[a])
+        def load_w8(g):
+            lo, hi = groups8[g]
+            nc.sync.dma_start(w8[g][:].bitcast(I32), v8[:, 2 * lo : 2 * hi, :].bitcast(I32))
 
-        def load_w(g):
-            nc.sync.dma_start(w8[g][:].bitcast(I32), v8[:, 4 * g : 4 * g + 4, :].bitcast(I32))
-            nc.sync.dma_start(w4[g][:].bitcast(I32), v4[:, 6 * g : 6 * g + 6, :].bitcast(I32))
+        def load_w4(g):
+            lo, hi = groups4[g]
+            nc.sync.dma_start(w4[g][:].bitcast(I32), v4[:, 3 * lo : 3 * hi, :].bitcast(I32))
 
-        load_x(2)
+        def weights(tiles, groups, e, i, n, m):
+            g = [lo <= e < hi for lo, hi in groups].index(True)
+            return tiles[g][:, n * (e - groups[g][0]) + i, m[0] : m[1]]
+
+        gates = {(c, h): keep.tile([P, T], F32, name=f"gate{c}{h}") for h in range(HALVES) for c in range(2)}
+
+        nc.sync.dma_start(raw[2][:], xv[2])
         nc.sync.dma_start(offs_t[:], offs)
-        load_x(3)
-        load_x(0)
-        load_w(0)
-        load_x(4)
-        load_x(1)
-        load_w(1)
-        load_w(2)
-        load_w(3)
+        bias = keep.tile([P, HALVES, E], F32, name="bias")
+        nc.sync.dma_start(raw[3][:], xv[3])
+        nc.sync.dma_start(raw[0][:], xv[0])
         nc.sync.dma_start(bias[:], b.rearrange("(h p) e -> p h e", p=P))
         nc.sync.dma_start(pos1_t[:], pos1)
         nc.sync.dma_start(pos2_t[:], pos2)
-        gates = {}
+        nc.sync.dma_start(raw[4][:], xv[4])
+        nc.sync.dma_start(raw[1][:], xv[1])
+        load_w4(0)
+        load_w8(0)
+        load_w4(1)
+        load_w8(1)
+        load_w4(2)
+        load_w8(2)
+        load_w4(3)
+        load_w8(3)
+        load_w4(4)
+        load_w8(4)
+        load_w4(5)
+        load_w8(5)
         for h in range(HALVES):
             for c in range(2):
-                gates[c, h] = keep.tile([P, T], F32, name=f"gate{c}{h}")
                 nc.sync.dma_start(gates[c, h][:], gate[c, h * P : (h + 1) * P, :])
 
         xb = {a: keep.tile([P, T, 4], BF16, name=f"xb{a}", align_bytes=64) for a in ORDER}
@@ -135,47 +151,43 @@ def tile_moe_rag_lin_gelu_kernel(
             quant(a, 0, 512)
             quant(a, 512, T)
 
-        pieces = ((0, 384), (384, 768), (768, 1152), (1152, 1280))
-
-        def gp(a, i):
-            gather(gwords[a], words[a], pieces[i][0], pieces[i][1])
+        pieces = ((0, 256), (256, 512), (512, 768), (768, 1024), (1024, 1152), (1152, 1280))
 
         cast(2, 0, 256)
         cast(2, 512, T, vector=True)
         cast(2, 256, 512, vector=True)
         cast(3, 0, 256)
-        cast(3, 256, 512)
-        for a in (0, 4):
-            cast(a, 0, 512)
-            cast(a, 512, T)
+        cast(3, 256, 448)
+        cast(0, 0, 512)
+        cast(0, 512, T)
+        cast(4, 0, 512)
 
         quant(2, 512, T)
         quant(2, 256, 512)
         quant(2, 0, 256)
         gw(2, 0)
         gw(2, 1)
-        cast(3, 512, T, vector=True)
+        cast(3, 448, T, vector=True)
         gw(2, 2)
         quant(3, 512, T)
         quant(3, 0, 512)
-        gw(3, 0)
-        gw(3, 1)
-        quant(0, 0, 512)
-        gw(3, 2)
-        quant(0, 512, T)
         for i in range(3):
             gather(gpacked, packed, thirds[i][0], thirds[i][1])
         nc.scalar.dma_start(gmoved[0:112, :].bitcast(I32), gpacked[8:120, :].bitcast(I32))
+        cast(4, 512, T)
         cast(1, 0, 512)
         cast(1, 512, T)
+        for i in range(2):
+            gw(3, i)
+        q(0)
+        gw(3, 2)
         gw(0, 0)
-        gw(0, 1)
         q(4)
+        gw(0, 1)
         gw(0, 2)
-        gp(4, 0)
-        gp(4, 1)
+        for i in range(1):
+            gather(gwords[4], words[4], pieces[i][0], pieces[i][1])
         q(1)
-        gp(4, 3)
 
         y = [keep.tile([P, SLOTS], F32, name=f"y{h}") for h in range(HALVES)]
         acc = {}
@@ -185,10 +197,10 @@ def tile_moe_rag_lin_gelu_kernel(
             s = blk * BLOCK
             cols = slice(s, s + BLOCK)
             if a < PASSES8:
-                lhsT = w8[e // 2][:, PASSES8 * (e % 2) + a, 512 * h : 512 * (h + 1)].bitcast(FP8X4)
+                lhsT = weights(w8, groups8, e, a, 2, (512 * h, 512 * (h + 1))).bitcast(FP8X4)
                 lhsT_scale = w8s[:, PASSES8 * e + a, h * P : (h + 1) * P]
             else:
-                lhsT = w4[e // 2][:, 3 * (e % 2) + a - PASSES8, 256 * h : 256 * (h + 1)].bitcast(FP4X4)
+                lhsT = weights(w4, groups4, e, a - PASSES8, 3, (256 * h, 256 * (h + 1))).bitcast(FP4X4)
                 lhsT_scale = w4s[:, 3 * e + a - PASSES8, h * P : (h + 1) * P]
             if a == MOVED:
                 rhs_scale = gmoved[:, cols]
@@ -204,11 +216,14 @@ def tile_moe_rag_lin_gelu_kernel(
                 stop=(a == ORDER[-1]),
             )
 
-        def begin(blk):
-            for h in range(HALVES):
-                acc[blk, h] = psum.tile([P, BLOCK], F32, name="acc")
-                for a in EARLY:
-                    multiply(blk, h, a)
+        def begin(blks):
+            for blk in blks:
+                for h in range(HALVES):
+                    acc[blk, h] = psum.tile([P, BLOCK], F32, name="acc")
+            for a in EARLY:
+                for blk in blks:
+                    for h in range(HALVES):
+                        multiply(blk, h, a)
 
         def finish(blk):
             e = BLOCK_EXPERT[blk]
@@ -218,21 +233,25 @@ def tile_moe_rag_lin_gelu_kernel(
                 s = blk * BLOCK
                 nc.scalar.activation(y[h][:, s : s + BLOCK], acc[blk, h][:], GELU, bias=bias[:, h, e : e + 1])
 
-        for blk in range(4):
-            begin(blk)
-        opened = 4
+        ahead = 3
+        begin(range(ahead))
+        opened = ahead
         for i, (lo, hi) in enumerate(pieces):
-            if i == 2:
-                gp(4, 2)
-            gather(glast, lastp, lo, hi)
-            gp(1, i)
+            if 1 <= i < 4:
+                gather(gwords[4], words[4], lo, hi)
+            if i < 4:
+                gather(glast, lastp, lo, hi)
+            elif i == 4:
+                gather(gwords[4], words[4], lo, SLOTS)
+                gather(glast, lastp, lo, SLOTS)
+            gather(gwords[1], words[1], lo, hi)
             for blk in range(lo // BLOCK, hi // BLOCK):
                 finish(blk)
-            while opened < min(len(BLOCK_EXPERT), hi // BLOCK + 4):
-                begin(opened)
-                opened += 1
+            nxt = max(opened, min(len(BLOCK_EXPERT), hi // BLOCK + ahead))
+            begin(range(opened, nxt))
+            opened = nxt
 
-        spans = ((0, 0, T), (1, 0, 320), (1, 320, T))
+        spans = ((0, 0, T), (1, 0, 512), (1, 512, T))
         prods = {}
 
         def product(i, c):

from contextlib import ExitStack

import concourse.mybir as mybir

P = 128
K, T, E, N = 2560, 640, 8, 256
COUNTS = (128, 128, 128, 128, 128, 256, 256, 128)
SLOTS = 2 * T
BLOCK = 128
BLOCK_EXPERT = [e for e in range(E) for i in range(COUNTS[e] // BLOCK)]
HALVES = N // P
PASSES = K // 512
PASSES8 = 2

F32 = mybir.dt.float32
BF16 = mybir.dt.bfloat16
I32 = mybir.dt.int32
U32 = mybir.dt.uint32
U16 = mybir.dt.uint16
U8 = mybir.dt.uint8
FP8X4 = mybir.dt.float8_e4m3fn_x4
FP4X4 = mybir.dt.float4_e2m1fn_x4
COPY = mybir.ActivationFunctionType.Copy
GELU = mybir.ActivationFunctionType.Gelu_apprx_tanh
MULT = mybir.AluOpType.mult

FLOPS = 2 * SLOTS * K * N

ORDER = (2, 3, 0, 4, 1)
EARLY = ORDER[:2]
LATE = ORDER[2:]
ROW = {2: 0, 3: 8, 4: 0, 0: 4, 1: 8}
MOVED = 3


def tile_moe_rag_lin_gelu_kernel(
    tc, xT, w8_words, w8_scales, w4_words, w4_scales, b, gate, offs, pos1, pos2, out
):
    nc = tc.nc
    with ExitStack() as ctx:
        lists = ctx.enter_context(tc.tile_pool(name="lists", bufs=1))
        keep = ctx.enter_context(tc.tile_pool(name="keep", bufs=1))
        psum = ctx.enter_context(tc.psum_pool(name="psum", bufs=8))

        offs_t = lists.tile([P, SLOTS // 16], U16, name="offs_t")
        pos1_t = lists.tile([P, T // 16], U16, name="pos1_t")
        pos2_t = lists.tile([P, T // 16], U16, name="pos2_t")

        w4s = keep.tile([P, E * (PASSES - PASSES8), N], U8, name="w4s", align_bytes=64)
        w8s = keep.tile([P, E * PASSES8, N], U8, name="w8s", align_bytes=64)
        nc.vector.memset(w4s[:].bitcast(I32), 0)
        nc.vector.memset(w8s[:].bitcast(I32), 0)
        s8v = w8_scales.rearrange("e a q n -> q (e a) n")
        s4v = w4_scales.rearrange("e a q n -> q (e a) n")
        for q in range(4):
            nc.gpsimd.dma_start(w4s[32 * q : 32 * q + 4, :, :].bitcast(I32), s4v[4 * q : 4 * q + 4, :, :].bitcast(I32))

        for q in range(4):
            nc.gpsimd.dma_start(w8s[32 * q : 32 * q + 4, :, :].bitcast(I32), s8v[4 * q : 4 * q + 4, :, :].bitcast(I32))

        warm = keep.tile([P, 8], F32, name="warm")
        nc.vector.memset(warm[:], 0.0)
        warmed = keep.tile([P, 8], F32, name="warmed")
        nc.scalar.activation(warmed[:], warm[:], GELU)

        packed = keep.tile([P, T], U8, name="packed", align_bytes=64)
        nc.vector.memset(packed[:].bitcast(I32), 0)
        lastp = keep.tile([P, T], U8, name="lastp", align_bytes=64)
        nc.vector.memset(lastp[:].bitcast(I32), 0)
        gmoved = keep.tile([P, SLOTS], U8, name="gmoved", align_bytes=64)
        nc.vector.memset(gmoved[:].bitcast(I32), 0)

        raw = {a: keep.tile([P, 4, T], F32, name=f"raw{a}") for a in ORDER}
        xv = xT.rearrange("(a p j) t -> a p j t", p=P, j=4)
        v8 = w8_words.rearrange("e a p n r -> p (e a) (n r)")
        v4 = w4_words.rearrange("e a p m -> p (e a) m")
        groups8 = ((0, 2), (2, 4), (4, 5), (5, 6), (6, 7), (7, 8))
        groups4 = ((0, 2), (2, 4), (4, 5), (5, 6), (6, 7), (7, 8))
        w8 = [keep.tile([P, 2 * (hi - lo), 4 * N], U8, name=f"w8_{lo}", align_bytes=64) for lo, hi in groups8]
        w4 = [keep.tile([P, 3 * (hi - lo), 2 * N], U8, name=f"w4_{lo}", align_bytes=64) for lo, hi in groups4]

        def load_w8(g):
            lo, hi = groups8[g]
            nc.sync.dma_start(w8[g][:].bitcast(I32), v8[:, 2 * lo : 2 * hi, :].bitcast(I32))

        def load_w4(g):
            lo, hi = groups4[g]
            nc.sync.dma_start(w4[g][:].bitcast(I32), v4[:, 3 * lo : 3 * hi, :].bitcast(I32))

        def weights(tiles, groups, e, i, n, m):
            g = [lo <= e < hi for lo, hi in groups].index(True)
            return tiles[g][:, n * (e - groups[g][0]) + i, m[0] : m[1]]

        gates = {(c, h): keep.tile([P, T], F32, name=f"gate{c}{h}") for h in range(HALVES) for c in range(2)}

        nc.sync.dma_start(raw[2][:], xv[2])
        nc.sync.dma_start(offs_t[:], offs)
        bias = keep.tile([P, HALVES, E], F32, name="bias")
        nc.sync.dma_start(raw[3][:], xv[3])
        nc.sync.dma_start(raw[0][:], xv[0])
        nc.sync.dma_start(bias[:], b.rearrange("(h p) e -> p h e", p=P))
        nc.sync.dma_start(pos1_t[:], pos1)
        nc.sync.dma_start(pos2_t[:], pos2)
        nc.sync.dma_start(raw[4][:], xv[4])
        nc.sync.dma_start(raw[1][:], xv[1])
        load_w4(0)
        load_w8(0)
        load_w4(1)
        load_w8(1)
        load_w4(2)
        load_w8(2)
        load_w4(3)
        load_w8(3)
        load_w4(4)
        load_w8(4)
        load_w4(5)
        load_w8(5)
        for h in range(HALVES):
            for c in range(2):
                nc.sync.dma_start(gates[c, h][:], gate[c, h * P : (h + 1) * P, :])

        xb = {a: keep.tile([P, T, 4], BF16, name=f"xb{a}", align_bytes=64) for a in ORDER}
        words = {a: keep.tile([P, T], U32, name=f"words{a}", align_bytes=64) for a in ORDER}
        gwords = {a: keep.tile([P, SLOTS], U32, name=f"gwords{a}", align_bytes=64) for a in ORDER}
        gpacked = keep.tile([P, SLOTS], U8, name="gpacked", align_bytes=64)
        glast = keep.tile([P, SLOTS], U8, name="glast", align_bytes=64)

        def cast(a, lo, hi, vector=False):
            dst = xb[a][:, lo:hi, :].rearrange("p (c i) t -> p c t i", i=4)
            src = raw[a][:, :, lo:hi].rearrange("p t (c i) -> p c t i", i=4)
            if vector:
                nc.vector.tensor_copy(dst, src)
            else:
                nc.scalar.activation(dst, src, COPY)

        def quant(a, lo, hi):
            scales = (packed if a in EARLY else lastp)[ROW[a] : P, lo:hi]
            nc.vector.quantize_mx(
                words[a][:, lo:hi].bitcast(FP8X4), scales, xb[a][:, lo:hi, :].rearrange("p c t -> p (c t)")
            )

        def gather(dst, window, lo, hi):
            nc.vector.tensor_copy(dst[:, lo:hi], window[:].indirect(offs_t[:, lo // 16 : hi // 16]))

        thirds = ((0, 480), (480, 960), (960, 1280))

        def gw(a, i):
            gather(gwords[a], words[a], thirds[i][0], thirds[i][1])

        def q(a):
            quant(a, 0, 512)
            quant(a, 512, T)

        pieces = ((0, 256), (256, 512), (512, 768), (768, 1024), (1024, 1152), (1152, 1280))

        cast(2, 0, 256)
        cast(2, 512, T, vector=True)
        cast(2, 256, 512, vector=True)
        cast(3, 0, 256)
        cast(3, 256, 448)
        cast(0, 0, 512)
        cast(0, 512, T)
        cast(4, 0, 512)

        quant(2, 512, T)
        quant(2, 256, 512)
        quant(2, 0, 256)
        gw(2, 0)
        gw(2, 1)
        cast(3, 448, T, vector=True)
        gw(2, 2)
        quant(3, 512, T)
        quant(3, 0, 512)
        for i in range(3):
            gather(gpacked, packed, thirds[i][0], thirds[i][1])
        nc.scalar.dma_start(gmoved[0:112, :].bitcast(I32), gpacked[8:120, :].bitcast(I32))
        cast(4, 512, T)
        cast(1, 0, 512)
        cast(1, 512, T)
        for i in range(2):
            gw(3, i)
        q(0)
        gw(3, 2)
        gw(0, 0)
        q(4)
        gw(0, 1)
        gw(0, 2)
        for i in range(1):
            gather(gwords[4], words[4], pieces[i][0], pieces[i][1])
        q(1)

        y = [keep.tile([P, SLOTS], F32, name=f"y{h}") for h in range(HALVES)]
        acc = {}

        def multiply(blk, h, a):
            e = BLOCK_EXPERT[blk]
            s = blk * BLOCK
            cols = slice(s, s + BLOCK)
            if a < PASSES8:
                lhsT = weights(w8, groups8, e, a, 2, (512 * h, 512 * (h + 1))).bitcast(FP8X4)
                lhsT_scale = w8s[:, PASSES8 * e + a, h * P : (h + 1) * P]
            else:
                lhsT = weights(w4, groups4, e, a - PASSES8, 3, (256 * h, 256 * (h + 1))).bitcast(FP4X4)
                lhsT_scale = w4s[:, 3 * e + a - PASSES8, h * P : (h + 1) * P]
            if a == MOVED:
                rhs_scale = gmoved[:, cols]
            else:
                rhs_scale = (gpacked if a in EARLY else glast)[ROW[a] : P, cols]
            nc.tensor.matmul_mx(
                acc[blk, h][:],
                lhsT=lhsT,
                lhsT_scale=lhsT_scale,
                rhs=gwords[a][:, cols].bitcast(FP8X4),
                rhs_scale=rhs_scale,
                start=(a == EARLY[0]),
                stop=(a == ORDER[-1]),
            )

        def begin(blks):
            for blk in blks:
                for h in range(HALVES):
                    acc[blk, h] = psum.tile([P, BLOCK], F32, name="acc")
            for a in EARLY:
                for blk in blks:
                    for h in range(HALVES):
                        multiply(blk, h, a)

        def finish(blk):
            e = BLOCK_EXPERT[blk]
            for h in range(HALVES):
                for a in LATE:
                    multiply(blk, h, a)
                s = blk * BLOCK
                nc.scalar.activation(y[h][:, s : s + BLOCK], acc[blk, h][:], GELU, bias=bias[:, h, e : e + 1])

        ahead = 3
        begin(range(ahead))
        opened = ahead
        for i, (lo, hi) in enumerate(pieces):
            if 1 <= i < 4:
                gather(gwords[4], words[4], lo, hi)
            if i < 4:
                gather(glast, lastp, lo, hi)
            elif i == 4:
                gather(gwords[4], words[4], lo, SLOTS)
                gather(glast, lastp, lo, SLOTS)
            gather(gwords[1], words[1], lo, hi)
            for blk in range(lo // BLOCK, hi // BLOCK):
                finish(blk)
            nxt = max(opened, min(len(BLOCK_EXPERT), hi // BLOCK + ahead))
            begin(range(opened, nxt))
            opened = nxt

        spans = ((0, 0, T), (1, 0, 512), (1, 512, T))
        prods = {}

        def product(i, c):
            h, lo, hi = spans[i]
            prods[i, c] = keep.tile([P, hi - lo], F32, name=f"prod{i}{c}")
            pos = (pos1_t, pos2_t)[c]
            nc.vector.tensor_tensor(prods[i, c][:], y[h][:].indirect(pos[:, lo // 16 : hi // 16]), gates[c, h][:, lo:hi], MULT)

        def combine(i):
            h, lo, hi = spans[i]
            res = keep.tile([P, hi - lo], F32, name=f"res{i}")
            nc.vector.tensor_add(res[:], prods[i, 0][:], prods[i, 1][:])
            nc.sync.dma_start(out[h * P : (h + 1) * P, lo:hi], res[:])

        product(0, 0)
        product(0, 1)
        product(1, 0)
        combine(0)
        product(1, 1)
        product(2, 0)
        combine(1)
        product(2, 1)
        combine(2)
